import numpy as np
import ml_dtypes

BF16 = ml_dtypes.bfloat16


def bf(x):
    return np.asarray(x, np.float32).astype(BF16)


def f32(x):
    return np.asarray(x, np.float32)


def f64(x):
    return np.asarray(x).astype(np.float64)


def striped(idx):
    return np.tile(idx.reshape(-1, 16).T, (8, 1))


S, K, M, N, D, V = 4096, 128, 256, 2048, 4, 512


def gelu_tanh(v):
    return 0.5 * v * (1.0 + np.tanh(np.sqrt(2.0 / np.pi) * (v + 0.044715 * v**3)))


def setup_inputs():
    return {"table": bf(np.random.standard_normal((K, S))), "w": bf(np.random.standard_normal((K, M)) / np.sqrt(K)), "b": f32(0.5 * np.random.standard_normal((M, 1))), "offs": striped(np.random.permutation(np.tile(np.arange(S), 2))[:N])}


def reference(table, w, b, offs):
    idx = offs[:16].T.reshape(-1)
    x = f64(table)[:, idx]
    y = f64(w).T @ x
    z = gelu_tanh(y + f64(b))
    return z.reshape(M, V, D).max(axis=2)

@@ -1,0 +1,51 @@
+import concourse.mybir as mybir
+
+BF16, F32, U16 = mybir.dt.bfloat16, mybir.dt.float32, mybir.dt.uint16
+GELU_TANH = mybir.ActivationFunctionType.Gelu_apprx_tanh
+
+P = 128
+S = 4096
+M = 256
+N = 2048
+GROUP = 4
+PIECE = 512
+PER_COLUMN = 16
+
+FLOPS = 2 * P * M * N
+
+
+def tile_gather_matmul_kernel(tc, table, w, b, offs, out):
+    nc = tc.nc
+    blocks = M // P
+    pieces = N // PIECE
+    pooled_columns = PIECE // GROUP
+    with (
+        tc.tile_pool(name="held", bufs=1) as held,
+        tc.tile_pool(name="work", bufs=4) as work,
+        tc.psum_pool(name="psum", bufs=blocks * pieces) as psum,
+    ):
+        offsets = held.tile([P, N // PER_COLUMN], U16, name="offsets")
+        nc.sync.dma_start(offsets[:], offs)
+        nodes = held.tile([P, S], BF16, name="nodes")
+        nc.sync.dma_start(nodes[:], table)
+        weights = held.tile([P, M], BF16, name="weights")
+        nc.scalar.dma_start(weights[:], w)
+        bias = held.tile([P, blocks], F32, name="bias")
+        with nc.allow_non_contiguous_dma(reason="256 single float32 values, one to a partition and block"):
+            nc.scalar.dma_start(bias[:], b.rearrange("(a p) o -> p (a o)", p=P))
+
+        for a in range(blocks):
+            for j in range(pieces):
+                product = psum.tile([P, PIECE], F32, name="product")
+                picked = nodes[:].indirect(offsets[:, j * PIECE // PER_COLUMN : (j + 1) * PIECE // PER_COLUMN])
+                nc.tensor.matmul(product[:], weights[:, a * P : (a + 1) * P], picked, start=True, stop=True)
+                active = work.tile([P, PIECE], F32, name="active")
+                nc.scalar.activation(active[:], product[:], GELU_TANH, bias=bias[:, a : a + 1])
+                pooled = work.tile([P, pooled_columns], F32, name="pooled")
+                nc.vector.tensor_reduce(
+                    pooled[:],
+                    active[:].rearrange("p (v t) -> p v t", t=GROUP),
+                    axis=mybir.AxisListType.X,
+                    op=mybir.AluOpType.max,
+                )
+                nc.sync.dma_start(out[a * P : (a + 1) * P, j * pooled_columns : (j + 1) * pooled_columns], pooled[:])

@@ -10,6 +10,8 @@ N = 2048
 GROUP = 4
 PIECE = 512
 PER_COLUMN = 16
+TABLE_LOADS = 2
+WARM_UP = 6
 
 FLOPS = 2 * P * M * N
 
@@ -26,13 +28,28 @@ def tile_gather_matmul_kernel(tc, table, w, b, offs, out):
     ):
         offsets = held.tile([P, N // PER_COLUMN], U16, name="offsets")
         nc.sync.dma_start(offsets[:], offs)
-        nodes = held.tile([P, S], BF16, name="nodes")
-        nc.sync.dma_start(nodes[:], table)
         weights = held.tile([P, M], BF16, name="weights")
         nc.scalar.dma_start(weights[:], w)
+        nodes = held.tile([P, S], BF16, name="nodes")
+        run = S // TABLE_LOADS
+        for r in range(TABLE_LOADS):
+            queue = nc.sync if r % 2 == 0 else nc.scalar
+            queue.dma_start(nodes[:, r * run : (r + 1) * run], table[:, r * run : (r + 1) * run])
         bias = held.tile([P, blocks], F32, name="bias")
         with nc.allow_non_contiguous_dma(reason="256 single float32 values, one to a partition and block"):
             nc.scalar.dma_start(bias[:], b.rearrange("(a p) o -> p (a o)", p=P))
+
+        scratch = held.tile([P, 1], F32, name="scratch")
+        nc.vector.memset(scratch[:], 0.0)
+        nc.scalar.activation(scratch[:], scratch[:], GELU_TANH)
+
+        zeros = held.tile([P, PIECE], BF16, name="zeros")
+        nc.vector.memset(zeros[:], 0.0)
+        unread = psum.tile([P, PIECE], F32, name="unread", tag="product")
+        for turn in range(WARM_UP):
+            nc.tensor.matmul(unread[:], zeros[:, :P], zeros[:], start=True, stop=True)
+
+        pooled = held.tile([P, blocks, N // GROUP], F32, name="pooled")
 
         for a in range(blocks):
             for j in range(pieces):
@@ -41,11 +58,11 @@ def tile_gather_matmul_kernel(tc, table, w, b, offs, out):
                 nc.tensor.matmul(product[:], weights[:, a * P : (a + 1) * P], picked, start=True, stop=True)
                 active = work.tile([P, PIECE], F32, name="active")
                 nc.scalar.activation(active[:], product[:], GELU_TANH, bias=bias[:, a : a + 1])
-                pooled = work.tile([P, pooled_columns], F32, name="pooled")
+                columns = slice(j * pooled_columns, (j + 1) * pooled_columns)
                 nc.vector.tensor_reduce(
-                    pooled[:],
+                    pooled[:, a, columns],
                     active[:].rearrange("p (v t) -> p v t", t=GROUP),
                     axis=mybir.AxisListType.X,
                     op=mybir.AluOpType.max,
                 )
-                nc.sync.dma_start(out[a * P : (a + 1) * P, j * pooled_columns : (j + 1) * pooled_columns], pooled[:])
+                nc.sync.dma_start(out[a * P : (a + 1) * P, columns], pooled[:, a, columns])

@@ -28,6 +28,9 @@ def tile_gather_matmul_kernel(tc, table, w, b, offs, out):
     ):
         offsets = held.tile([P, N // PER_COLUMN], U16, name="offsets")
         nc.sync.dma_start(offsets[:], offs)
+        bias = held.tile([P, blocks], F32, name="bias")
+        with nc.allow_non_contiguous_dma(reason="256 single float32 values, one to a partition and block"):
+            nc.sync.dma_start(bias[:], b.rearrange("(a p) o -> p (a o)", p=P))
         weights = held.tile([P, M], BF16, name="weights")
         nc.scalar.dma_start(weights[:], w)
         nodes = held.tile([P, S], BF16, name="nodes")
@@ -35,9 +38,6 @@ def tile_gather_matmul_kernel(tc, table, w, b, offs, out):
         for r in range(TABLE_LOADS):
             queue = nc.sync if r % 2 == 0 else nc.scalar
             queue.dma_start(nodes[:, r * run : (r + 1) * run], table[:, r * run : (r + 1) * run])
-        bias = held.tile([P, blocks], F32, name="bias")
-        with nc.allow_non_contiguous_dma(reason="256 single float32 values, one to a partition and block"):
-            nc.scalar.dma_start(bias[:], b.rearrange("(a p) o -> p (a o)", p=P))
 
         scratch = held.tile([P, 1], F32, name="scratch")
         nc.vector.memset(scratch[:], 0.0)

@@ -28,9 +28,6 @@ def tile_gather_matmul_kernel(tc, table, w, b, offs, out):
     ):
         offsets = held.tile([P, N // PER_COLUMN], U16, name="offsets")
         nc.sync.dma_start(offsets[:], offs)
-        bias = held.tile([P, blocks], F32, name="bias")
-        with nc.allow_non_contiguous_dma(reason="256 single float32 values, one to a partition and block"):
-            nc.sync.dma_start(bias[:], b.rearrange("(a p) o -> p (a o)", p=P))
         weights = held.tile([P, M], BF16, name="weights")
         nc.scalar.dma_start(weights[:], w)
         nodes = held.tile([P, S], BF16, name="nodes")
@@ -38,6 +35,9 @@ def tile_gather_matmul_kernel(tc, table, w, b, offs, out):
         for r in range(TABLE_LOADS):
             queue = nc.sync if r % 2 == 0 else nc.scalar
             queue.dma_start(nodes[:, r * run : (r + 1) * run], table[:, r * run : (r + 1) * run])
+        bias = held.tile([P, blocks], F32, name="bias")
+        with nc.allow_non_contiguous_dma(reason="256 single float32 values, one to a partition and block"):
+            nc.scalar.dma_start(bias[:], b.rearrange("(a p) o -> p (a o)", p=P))
 
         scratch = held.tile([P, 1], F32, name="scratch")
         nc.vector.memset(scratch[:], 0.0)
@@ -58,11 +58,9 @@ def tile_gather_matmul_kernel(tc, table, w, b, offs, out):
                 nc.tensor.matmul(product[:], weights[:, a * P : (a + 1) * P], picked, start=True, stop=True)
                 active = work.tile([P, PIECE], F32, name="active")
                 nc.scalar.activation(active[:], product[:], GELU_TANH, bias=bias[:, a : a + 1])
+                groups = active[:].rearrange("p (v t) -> p v t", t=GROUP)
+                pairs = work.tile([P, pooled_columns, GROUP // 2], F32, name="pairs")
+                nc.vector.tensor_max(pairs[:], groups[:, :, 0 : GROUP // 2], groups[:, :, GROUP // 2 : GROUP])
                 columns = slice(j * pooled_columns, (j + 1) * pooled_columns)
-                nc.vector.tensor_reduce(
-                    pooled[:, a, columns],
-                    active[:].rearrange("p (v t) -> p v t", t=GROUP),
-                    axis=mybir.AxisListType.X,
-                    op=mybir.AluOpType.max,
-                )
+                nc.vector.tensor_max(pooled[:, a, columns], pairs[:, :, 0], pairs[:, :, 1])
                 nc.sync.dma_start(out[a * P : (a + 1) * P, columns], pooled[:, a, columns])

@@ -11,7 +11,6 @@ GROUP = 4
 PIECE = 512
 PER_COLUMN = 16
 TABLE_LOADS = 2
-WARM_UP = 6
 
 FLOPS = 2 * P * M * N
 
@@ -43,12 +42,6 @@ def tile_gather_matmul_kernel(tc, table, w, b, offs, out):
         nc.vector.memset(scratch[:], 0.0)
         nc.scalar.activation(scratch[:], scratch[:], GELU_TANH)
 
-        zeros = held.tile([P, PIECE], BF16, name="zeros")
-        nc.vector.memset(zeros[:], 0.0)
-        unread = psum.tile([P, PIECE], F32, name="unread", tag="product")
-        for turn in range(WARM_UP):
-            nc.tensor.matmul(unread[:], zeros[:, :P], zeros[:], start=True, stop=True)
-
         pooled = held.tile([P, blocks, N // GROUP], F32, name="pooled")
 
         for a in range(blocks):
@@ -58,9 +51,11 @@ def tile_gather_matmul_kernel(tc, table, w, b, offs, out):
                 nc.tensor.matmul(product[:], weights[:, a * P : (a + 1) * P], picked, start=True, stop=True)
                 active = work.tile([P, PIECE], F32, name="active")
                 nc.scalar.activation(active[:], product[:], GELU_TANH, bias=bias[:, a : a + 1])
-                groups = active[:].rearrange("p (v t) -> p v t", t=GROUP)
-                pairs = work.tile([P, pooled_columns, GROUP // 2], F32, name="pairs")
-                nc.vector.tensor_max(pairs[:], groups[:, :, 0 : GROUP // 2], groups[:, :, GROUP // 2 : GROUP])
                 columns = slice(j * pooled_columns, (j + 1) * pooled_columns)
-                nc.vector.tensor_max(pooled[:, a, columns], pairs[:, :, 0], pairs[:, :, 1])
+                nc.vector.tensor_reduce(
+                    pooled[:, a, columns],
+                    active[:].rearrange("p (v t) -> p v t", t=GROUP),
+                    axis=mybir.AxisListType.X,
+                    op=mybir.AluOpType.max,
+                )
                 nc.sync.dma_start(out[a * P : (a + 1) * P, columns], pooled[:, a, columns])

@@ -8,7 +8,8 @@ S = 4096
 M = 256
 N = 2048
 GROUP = 4
-PIECE = 512
+PIECE = 256
+BANKS = 8
 PER_COLUMN = 16
 TABLE_LOADS = 2
 
@@ -23,7 +24,7 @@ def tile_gather_matmul_kernel(tc, table, w, b, offs, out):
     with (
         tc.tile_pool(name="held", bufs=1) as held,
         tc.tile_pool(name="work", bufs=4) as work,
-        tc.psum_pool(name="psum", bufs=blocks * pieces) as psum,
+        tc.psum_pool(name="psum", bufs=BANKS) as psum,
     ):
         offsets = held.tile([P, N // PER_COLUMN], U16, name="offsets")
         nc.sync.dma_start(offsets[:], offs)

@@ -23,7 +23,6 @@ def tile_gather_matmul_kernel(tc, table, w, b, offs, out):
     pooled_columns = PIECE // GROUP
     with (
         tc.tile_pool(name="held", bufs=1) as held,
-        tc.tile_pool(name="work", bufs=4) as work,
         tc.psum_pool(name="psum", bufs=BANKS) as psum,
     ):
         offsets = held.tile([P, N // PER_COLUMN], U16, name="offsets")
@@ -43,6 +42,7 @@ def tile_gather_matmul_kernel(tc, table, w, b, offs, out):
         nc.vector.memset(scratch[:], 0.0)
         nc.scalar.activation(scratch[:], scratch[:], GELU_TANH)
 
+        active = held.tile([P, blocks, N], F32, name="active")
         pooled = held.tile([P, blocks, N // GROUP], F32, name="pooled")
 
         for a in range(blocks):
@@ -50,12 +50,12 @@ def tile_gather_matmul_kernel(tc, table, w, b, offs, out):
                 product = psum.tile([P, PIECE], F32, name="product")
                 picked = nodes[:].indirect(offsets[:, j * PIECE // PER_COLUMN : (j + 1) * PIECE // PER_COLUMN])
                 nc.tensor.matmul(product[:], weights[:, a * P : (a + 1) * P], picked, start=True, stop=True)
-                active = work.tile([P, PIECE], F32, name="active")
-                nc.scalar.activation(active[:], product[:], GELU_TANH, bias=bias[:, a : a + 1])
+                entries = slice(j * PIECE, (j + 1) * PIECE)
+                nc.scalar.activation(active[:, a, entries], product[:], GELU_TANH, bias=bias[:, a : a + 1])
                 columns = slice(j * pooled_columns, (j + 1) * pooled_columns)
                 nc.vector.tensor_reduce(
                     pooled[:, a, columns],
-                    active[:].rearrange("p (v t) -> p v t", t=GROUP),
+                    active[:, a, entries].rearrange("p (v t) -> p v t", t=GROUP),
                     axis=mybir.AxisListType.X,
                     op=mybir.AluOpType.max,
                 )

import concourse.mybir as mybir

BF16, F32, U16 = mybir.dt.bfloat16, mybir.dt.float32, mybir.dt.uint16
GELU_TANH = mybir.ActivationFunctionType.Gelu_apprx_tanh

P = 128
S = 4096
M = 256
N = 2048
GROUP = 4
PIECE = 256
BANKS = 8
PER_COLUMN = 16
TABLE_LOADS = 2

FLOPS = 2 * P * M * N


def tile_gather_matmul_kernel(tc, table, w, b, offs, out):
    nc = tc.nc
    blocks = M // P
    pieces = N // PIECE
    pooled_columns = PIECE // GROUP
    with (
        tc.tile_pool(name="held", bufs=1) as held,
        tc.psum_pool(name="psum", bufs=BANKS) as psum,
    ):
        offsets = held.tile([P, N // PER_COLUMN], U16, name="offsets")
        nc.sync.dma_start(offsets[:], offs)
        weights = held.tile([P, M], BF16, name="weights")
        nc.scalar.dma_start(weights[:], w)
        nodes = held.tile([P, S], BF16, name="nodes")
        run = S // TABLE_LOADS
        for r in range(TABLE_LOADS):
            queue = nc.sync if r % 2 == 0 else nc.scalar
            queue.dma_start(nodes[:, r * run : (r + 1) * run], table[:, r * run : (r + 1) * run])
        bias = held.tile([P, blocks], F32, name="bias")
        with nc.allow_non_contiguous_dma(reason="256 single float32 values, one to a partition and block"):
            nc.scalar.dma_start(bias[:], b.rearrange("(a p) o -> p (a o)", p=P))

        scratch = held.tile([P, 1], F32, name="scratch")
        nc.vector.memset(scratch[:], 0.0)
        nc.scalar.activation(scratch[:], scratch[:], GELU_TANH)

        active = held.tile([P, blocks, N], F32, name="active")
        pooled = held.tile([P, blocks, N // GROUP], F32, name="pooled")

        for a in range(blocks):
            for j in range(pieces):
                product = psum.tile([P, PIECE], F32, name="product")
                picked = nodes[:].indirect(offsets[:, j * PIECE // PER_COLUMN : (j + 1) * PIECE // PER_COLUMN])
                nc.tensor.matmul(product[:], weights[:, a * P : (a + 1) * P], picked, start=True, stop=True)
                entries = slice(j * PIECE, (j + 1) * PIECE)
                nc.scalar.activation(active[:, a, entries], product[:], GELU_TANH, bias=bias[:, a : a + 1])
                columns = slice(j * pooled_columns, (j + 1) * pooled_columns)
                nc.vector.tensor_reduce(
                    pooled[:, a, columns],
                    active[:, a, entries].rearrange("p (v t) -> p v t", t=GROUP),
                    axis=mybir.AxisListType.X,
                    op=mybir.AluOpType.max,
                )
                nc.sync.dma_start(out[a * P : (a + 1) * P, columns], pooled[:, a, columns])
